import numpy as np
import ml_dtypes


def mxq(x, axis, fmt="e4m3"):
    dtype, down = {"e4m3": (ml_dtypes.float8_e4m3fn, 7), "e5m2": (ml_dtypes.float8_e5m2, 14)}[fmt]
    v = np.moveaxis(np.asarray(x, np.float32).astype(ml_dtypes.bfloat16).astype(np.float64), axis, -1)
    blocks = v.reshape(v.shape[:-1] + (-1, 32))
    amax = np.abs(blocks).max(-1, keepdims=True)
    byte = np.maximum(np.where(amax > 0, np.frexp(amax)[1] - 1 + 127, 0) - down, 1)
    scale = np.exp2(byte - 127.0)
    codes = (blocks / scale).astype(np.float32).astype(dtype).astype(np.float64)
    return np.moveaxis((codes * scale).reshape(v.shape), -1, axis)


WIDE = False


def mx_kscale(k):
    if not WIDE:
        return np.ones(k)
    levels = np.array([10, -10, 5, -5, 0])
    if k % 512:
        return np.exp2(np.random.permutation(np.resize(levels, k // 32))).repeat(32)
    a = np.empty((k // 512, 16))
    for p in range(k // 512):
        a[p, :8] = np.random.permutation(np.resize(levels, 8))
        for g in range(8):
            far = levels[np.abs(levels - a[p, g]) >= 10]
            a[p, g + 8] = far[np.random.randint(len(far))]
    return np.exp2(a.ravel()).repeat(32)


def f64(x):
    return np.asarray(x).astype(np.float64)


def striped(idx):
    return np.tile(np.asarray(idx).reshape(-1, 16).T, (8, 1)).astype(np.uint16)


def unstriped(offs):
    return offs[:16].T.reshape(-1).astype(np.int64)


E2M1 = np.array([0.0, 0.5, 1.0, 1.5, 2.0, 3.0, 4.0, 6.0, -0.0, -0.5, -1.0, -1.5, -2.0, -3.0, -4.0, -6.0])


def pack_weight(w, fmt):
    k, n = w.shape
    w = f64(np.asarray(w, np.float32).astype(ml_dtypes.bfloat16)).reshape(k // 32, 32, n)
    amax = np.abs(w).max(1)
    if fmt == "e4m3":
        byte = np.frexp(amax)[1] - 1 + 127 - 7
    else:
        mant, ex = np.frexp(amax / 6.0)
        byte = np.where(mant > 0.5, ex, ex - 1) + 127
    byte = np.clip(np.where(amax > 0, byte, 1), 1, 254)
    scaled = (w * np.exp2(127.0 - byte)[:, None, :]).reshape(k, n).astype(np.float32)
    by_word = np.ascontiguousarray(scaled.reshape(k // 512, 128, 4, n).transpose(0, 1, 3, 2))
    if fmt == "e4m3":
        words = by_word.astype(ml_dtypes.float8_e4m3fn).view(np.uint8)
    else:
        c = by_word.astype(ml_dtypes.float4_e2m1fn).view(np.uint8) & 0xF
        words = (c[..., 0::2] | (c[..., 1::2] << 4)).reshape(k // 512, 128, 2 * n)
    return np.ascontiguousarray(words), np.ascontiguousarray(byte.astype(np.uint8).reshape(k // 512, 16, n))


def unpack_weight(words, scales, fmt):
    g, _, n = scales.shape
    words = np.ascontiguousarray(words).reshape(g, 128, n, -1)
    if fmt == "e4m3":
        vals = words.view(ml_dtypes.float8_e4m3fn).astype(np.float64)
    else:
        nib = np.empty((g, 128, n, 4), np.uint8)
        nib[..., 0::2] = words & 0xF
        nib[..., 1::2] = words >> 4
        vals = E2M1[nib]
    vals = vals * np.repeat(np.exp2(scales.astype(np.float64) - 127.0), 8, axis=1)[..., None]
    return vals.transpose(0, 1, 3, 2).reshape(g * 512, n)


def bf(x):
    return np.asarray(x, np.float32).astype(ml_dtypes.bfloat16)


def planes(Y):
    r, m = Y.shape
    b = f64(bf(Y)).reshape(r // 32, 32, m)
    amax = np.abs(b).max(1)
    byte = np.clip(np.where(amax > 0, np.frexp(amax)[1] - 1 + 127 - 7, 1), 1, 254)
    codes = (b * np.exp2(127.0 - byte)[:, None, :]).reshape(r, m).astype(np.float32).astype(ml_dtypes.float8_e4m3fn).view(np.uint8)
    words = codes.reshape(r // 512, 128, 4, m).transpose(0, 1, 3, 2)
    return np.ascontiguousarray(words), np.ascontiguousarray(byte.astype(np.uint8).reshape(r // 512, 16, m))


K, T, J, N = 512, 512, 512, 512


def setup_inputs():
    n = np.random.standard_normal
    idx = np.random.randint(0, T, J)
    idx2 = np.random.randint(0, T, J)
    fk = mx_kscale(K)
    wap = pack_weight(n((K, N)) * 1 / np.sqrt(K) * fk[:, None], "e4m3")
    wbp = pack_weight(n((K, N)) * 1 / np.sqrt(K) * fk[:, None], "e2m1")
    return {
        "xt": (n((K, T)) / fk[:, None]).astype(np.float32),
        "wa_words": wap[0],
        "wa_scales": wap[1],
        "wb_words": wbp[0],
        "wb_scales": wbp[1],
        "offs": striped(idx),
        "offs2": striped(idx2),
    }


def reference(xt, wa_words, wa_scales, wb_words, wb_scales, offs, offs2):
    idx = unstriped(offs)
    idx2 = unstriped(offs2)
    wau = unpack_weight(wa_words, wa_scales, "e4m3")
    wbu = unpack_weight(wb_words, wb_scales, "e2m1")
    xtq = mxq(f64(xt), 0, "e4m3")
    za = wau.T @ xtq
    zb = wbu.T @ xtq
    d = za[:, idx] - zb[:, idx2]
    y = np.square(d) / (1.0 + np.abs(d))
    words, scales = planes(y)
    return y, words, scales

@@ -1,0 +1,195 @@
+from contextlib import ExitStack
+
+import concourse.mybir as mybir
+
+K, T, J, N = 512, 512, 512, 512
+FLOPS = 2 * 2 * K * T * N
+
+F32 = mybir.dt.float32
+BF16 = mybir.dt.bfloat16
+I32 = mybir.dt.int32
+U32 = mybir.dt.uint32
+U16 = mybir.dt.uint16
+U8 = mybir.dt.uint8
+FP8X4 = mybir.dt.float8_e4m3fn_x4
+FP4X4 = mybir.dt.float4_e2m1fn_x4
+ACT = mybir.ActivationFunctionType
+ALU = mybir.AluOpType
+
+P = 128
+PACK = 4
+NODE_CHUNKS = (256, 128, 128)
+
+
+def spans(widths):
+    return [slice(sum(widths[:c]), sum(widths[: c + 1])) for c in range(len(widths))]
+
+
+def tile_list_edge_difference_energy_pl_kernel(
+    tc, xt, wa_words, wa_scales, wb_words, wb_scales, offs, offs2, out_0, out_1, out_2
+):
+    nc = tc.nc
+    with ExitStack() as ctx:
+        keep = ctx.enter_context(tc.tile_pool(name="keep", bufs=1))
+        psum = ctx.enter_context(tc.psum_pool(name="psum", bufs=8))
+
+        tails = keep.tile([P, J // 16], U16, name="tails")
+        heads = keep.tile([P, J // 16], U16, name="heads")
+
+        sa_raw = keep.tile([P, N], U8, name="sa_raw", align_bytes=64)
+        sb_raw = keep.tile([P, N], U8, name="sb_raw", align_bytes=64)
+        nc.gpsimd.memset(sb_raw[:].bitcast(I32), 0)
+        nc.gpsimd.memset(sa_raw[:].bitcast(I32), 0)
+
+        one = keep.tile([P, 1], F32, name="one")
+        warm = keep.tile([P, 1], F32, name="warm")
+        nc.gpsimd.memset(one[:], 1.0)
+
+        x_rows = xt.rearrange("(p i) t -> p i t", i=PACK)
+        node_spans = spans(NODE_CHUNKS)
+        x_raw = [keep.tile([P, PACK, w], F32, name=f"x_raw{h}") for h, w in enumerate(NODE_CHUNKS)]
+        wa_raw = keep.tile([P, N], I32, name="wa_raw")
+        wb_raw = keep.tile([P, 2 * N], U8, name="wb_raw")
+
+        nc.sync.dma_start(wb_raw[:].bitcast(I32), wb_words[0].bitcast(I32))
+        nc.sync.dma_start(heads[:], offs2)
+        nc.sync.dma_start(tails[:], offs)
+        for q in range(4):
+            nc.scalar.dma_start(sb_raw[32 * q : 32 * q + 4, :].bitcast(I32), wb_scales[0, 4 * q : 4 * q + 4, :].bitcast(I32))
+        for h, cols in enumerate(node_spans):
+            nc.sync.dma_start(x_raw[h][:], x_rows[:, :, cols])
+        nc.scalar.activation(warm[:], one[:], ACT.Abs_reciprocal_sqrt)
+        nc.sync.dma_start(wa_raw[:], wa_words[0].rearrange("p n r -> p (n r)").bitcast(I32))
+        for q in range(4):
+            nc.scalar.dma_start(sa_raw[32 * q : 32 * q + 4, :].bitcast(I32), wa_scales[0, 4 * q : 4 * q + 4, :].bitcast(I32))
+
+        wa = keep.tile([P, PACK, P], I32, name="wa", align_bytes=64)
+        wb = keep.tile([P, PACK, P, 2], U8, name="wb", align_bytes=64)
+        sa = keep.tile([P, PACK, P], U8, name="sa", align_bytes=64)
+        sb = keep.tile([P, PACK, P], U8, name="sb", align_bytes=64)
+        x_codes = keep.tile([P, T], U32, name="x_codes", align_bytes=64)
+        x_scales = keep.tile([P, T], U8, name="x_scales", align_bytes=64)
+        x_bf = [keep.tile([P, w, PACK], BF16, name=f"x_bf{h}", align_bytes=64) for h, w in enumerate(NODE_CHUNKS)]
+
+        nc.vector.tensor_copy(wb[:], wb_raw[:].rearrange("p (q r b) -> p r q b", r=PACK, b=2))
+        nc.vector.tensor_copy(sb[:], sb_raw[:].rearrange("p (q r) -> p r q", r=PACK))
+        for h, cols in enumerate(node_spans):
+            nc.vector.tensor_copy(x_bf[h][:], x_raw[h][:].rearrange("p i t -> p t i"))
+            nc.vector.quantize_mx(
+                out=x_codes[:, cols].bitcast(FP8X4), scales=x_scales[:, cols], in_=x_bf[h][:].rearrange("p t i -> p (t i)")
+            )
+        nc.vector.tensor_copy(wa[:], wa_raw[:].rearrange("p (q r) -> p r q", r=PACK))
+        nc.vector.tensor_copy(sa[:], sa_raw[:].rearrange("p (q r) -> p r q", r=PACK))
+
+        za = [keep.tile([P, T], F32, name=f"za{r}") for r in range(PACK)]
+        zb = keep.tile([P, PACK, T], F32, name="zb")
+
+        def product(out, words, scales, cols):
+            nc.tensor.matmul_mx(
+                out=out,
+                lhsT=words,
+                lhsT_scale=scales,
+                rhs=x_codes[:, cols].bitcast(FP8X4),
+                rhs_scale=x_scales[:, cols],
+                start=True,
+                stop=True,
+            )
+
+        wa_words_of = [wa[:, r, :].bitcast(FP8X4) for r in range(PACK)]
+        wb_words_of = [wb[:, r].rearrange("p q b -> p (q b)").bitcast(FP4X4) for r in range(PACK)]
+        for h, cols in enumerate(node_spans):
+            w = cols.stop - cols.start
+            per_bank = 1 if h == len(NODE_CHUNKS) - 1 else T // w
+            for r0 in range(0, PACK, per_bank):
+                bank = psum.tile([P, per_bank, w], F32, name="bank")
+                for i in range(per_bank):
+                    product(bank[:, i, :], wb_words_of[r0 + i], sb[:, r0 + i, :], cols)
+                nc.scalar.copy(zb[:, r0 : r0 + per_bank, cols], bank[:])
+        last = node_spans[-1]
+        for r in range(PACK):
+            bank = psum.tile([P, last.start], F32, name="bank")
+            for cols in node_spans[:-1]:
+                product(bank[:, cols], wa_words_of[r], sa[:, r, :], cols)
+            nc.scalar.copy(za[r][:, 0 : last.start], bank[:])
+        bank = psum.tile([P, PACK, T - last.start], F32, name="bank")
+        for r in range(PACK):
+            product(bank[:, r, :], wa_words_of[r], sa[:, r, :], last)
+        for r in range(PACK):
+            nc.scalar.copy(za[r][:, last], bank[:, r, :])
+
+        y_codes = keep.tile([P, J], U32, name="y_codes", align_bytes=64)
+        y_scales = keep.tile([P, J], U8, name="y_scales", align_bytes=64)
+        y_rows = out_0.rearrange("(p r) j -> p r j", r=PACK)
+        code_rows = out_1[0].rearrange("p j r -> p (j r)").bitcast(I32)
+
+        def block(name):
+            return keep.tile([P, PACK, P], F32, name=name)
+
+        def pick(out, b0, nb):
+            for r in range(PACK):
+                nc.vector.tensor_copy(out[:, r, :], zb[:, r, :].indirect(heads[:, 8 * b0 : 8 * (b0 + nb)]))
+
+        def differ(d, picked, b):
+            for r in range(PACK):
+                nc.vector.tensor_tensor(d[:, r, :], za[r][:].indirect(tails[:, 8 * b : 8 * (b + 1)]), picked[:, r, :], ALU.subtract)
+
+        def soften(b, d, groups):
+            a = block(f"a{b}")
+            s = block(f"s{b}")
+            for rows in groups:
+                nc.scalar.activation(a[:, rows, :], d[:, rows, :], ACT.Abs)
+                nc.scalar.activation(s[:, rows, :], a[:, rows, :], ACT.Abs_reciprocal_sqrt, bias=1.0)
+            return s
+
+        def scale(b, d, s, groups):
+            v = block(f"v{b}")
+            for rows in groups:
+                nc.vector.tensor_tensor(v[:, rows, :], d[:, rows, :], s[:, rows, :], ALU.mult)
+            return v
+
+        def planes(b, v):
+            edges = slice(P * b, P * (b + 1))
+            y_bf = keep.tile([P, P, PACK], BF16, name=f"y_bf{b}", align_bytes=64)
+            nc.scalar.activation(y_bf[:], v[:].rearrange("p r j -> p j r"), ACT.Square)
+            nc.vector.quantize_mx(
+                out=y_codes[:, edges].bitcast(FP8X4), scales=y_scales[:, edges], in_=y_bf[:].rearrange("p j r -> p (j r)")
+            )
+            nc.sync.dma_start(code_rows[:, edges], y_codes[:, edges].bitcast(I32))
+
+        def energy(b, v, on_vector):
+            y = block(f"y{b}")
+            if on_vector:
+                nc.vector.tensor_tensor(y[:], v[:], v[:], ALU.mult)
+            else:
+                nc.scalar.activation(y[:], v[:], ACT.Square)
+            nc.sync.dma_start(y_rows[:, :, P * b : P * (b + 1)], y[:])
+
+        whole = [slice(0, PACK)]
+        split = [slice(0, PACK - 1), slice(PACK - 1, PACK)]
+        p01 = keep.tile([P, PACK, 2 * P], F32, name="p01")
+        d0, d1, d3 = block("d0"), block("d1"), block("d3")
+        pick(p01, 0, 2)
+        differ(d0, p01[:, :, 0:P], 0)
+        s0 = soften(0, d0, whole)
+        differ(d1, p01[:, :, P : 2 * P], 1)
+        s1 = soften(1, d1, whole)
+        v0 = scale(0, d0, s0, whole)
+        planes(0, v0)
+        energy(0, v0, False)
+        pick(s0, 2, 1)
+        v1 = scale(1, d1, s1, whole)
+        planes(1, v1)
+        energy(1, v1, False)
+        differ(s1, s0, 2)
+        s2 = soften(2, s1, whole)
+        pick(s0, 3, 1)
+        differ(d3, s0, 3)
+        s3 = soften(3, d3, split)
+        v2 = scale(2, s1, s2, whole)
+        v3 = scale(3, d3, s3, split)
+        planes(2, v2)
+        planes(3, v3)
+        energy(3, v3, True)
+        energy(2, v2, True)
+        for q in range(4):
+            nc.scalar.dma_start(out_2[0, 4 * q : 4 * q + 4, :].bitcast(I32), y_scales[32 * q : 32 * q + 4, :].bitcast(I32))

@@ -1,6 +1,7 @@
 from contextlib import ExitStack
 
 import concourse.mybir as mybir
+from concourse.masks import make_identity
 
 K, T, J, N = 512, 512, 512, 512
 FLOPS = 2 * 2 * K * T * N
@@ -18,7 +19,9 @@ ALU = mybir.AluOpType
 
 P = 128
 PACK = 4
-NODE_CHUNKS = (256, 128, 128)
+SLABS = N // P
+BLOCKS = J // P
+NODE_CHUNKS = (128, 128, 128, 128)
 
 
 def spans(widths):
@@ -36,160 +39,166 @@ def tile_list_edge_difference_energy_pl_kernel(
         tails = keep.tile([P, J // 16], U16, name="tails")
         heads = keep.tile([P, J // 16], U16, name="heads")
 
-        sa_raw = keep.tile([P, N], U8, name="sa_raw", align_bytes=64)
-        sb_raw = keep.tile([P, N], U8, name="sb_raw", align_bytes=64)
-        nc.gpsimd.memset(sb_raw[:].bitcast(I32), 0)
-        nc.gpsimd.memset(sa_raw[:].bitcast(I32), 0)
+        sa = keep.tile([P, N], U8, name="sa", align_bytes=64)
+        sb = keep.tile([P, N], U8, name="sb", align_bytes=64)
 
         one = keep.tile([P, 1], F32, name="one")
         warm = keep.tile([P, 1], F32, name="warm")
         nc.gpsimd.memset(one[:], 1.0)
+        ident = keep.tile([P, P], F32, name="ident")
+        make_identity(nc, ident[:])
 
         x_rows = xt.rearrange("(p i) t -> p i t", i=PACK)
         node_spans = spans(NODE_CHUNKS)
         x_raw = [keep.tile([P, PACK, w], F32, name=f"x_raw{h}") for h, w in enumerate(NODE_CHUNKS)]
-        wa_raw = keep.tile([P, N], I32, name="wa_raw")
-        wb_raw = keep.tile([P, 2 * N], U8, name="wb_raw")
+        wa = keep.tile([P, N], I32, name="wa", align_bytes=64)
+        wb = keep.tile([P, 2 * N], U8, name="wb", align_bytes=64)
 
-        nc.sync.dma_start(wb_raw[:].bitcast(I32), wb_words[0].bitcast(I32))
-        nc.sync.dma_start(heads[:], offs2)
-        nc.sync.dma_start(tails[:], offs)
+        nc.sync.dma_start(wb[:].bitcast(I32), wb_words[0].bitcast(I32))
         for q in range(4):
-            nc.scalar.dma_start(sb_raw[32 * q : 32 * q + 4, :].bitcast(I32), wb_scales[0, 4 * q : 4 * q + 4, :].bitcast(I32))
+            nc.scalar.dma_start(sb[32 * q : 32 * q + 4, :].bitcast(I32), wb_scales[0, 4 * q : 4 * q + 4, :].bitcast(I32))
         for h, cols in enumerate(node_spans):
             nc.sync.dma_start(x_raw[h][:], x_rows[:, :, cols])
         nc.scalar.activation(warm[:], one[:], ACT.Abs_reciprocal_sqrt)
-        nc.sync.dma_start(wa_raw[:], wa_words[0].rearrange("p n r -> p (n r)").bitcast(I32))
+        nc.sync.dma_start(wa[:], wa_words[0].rearrange("p n r -> p (n r)").bitcast(I32))
+        nc.sync.dma_start(heads[:], offs2)
         for q in range(4):
-            nc.scalar.dma_start(sa_raw[32 * q : 32 * q + 4, :].bitcast(I32), wa_scales[0, 4 * q : 4 * q + 4, :].bitcast(I32))
+            nc.sync.dma_start(sa[32 * q : 32 * q + 4, :].bitcast(I32), wa_scales[0, 4 * q : 4 * q + 4, :].bitcast(I32))
+        nc.sync.dma_start(tails[:], offs)
 
-        wa = keep.tile([P, PACK, P], I32, name="wa", align_bytes=64)
-        wb = keep.tile([P, PACK, P, 2], U8, name="wb", align_bytes=64)
-        sa = keep.tile([P, PACK, P], U8, name="sa", align_bytes=64)
-        sb = keep.tile([P, PACK, P], U8, name="sb", align_bytes=64)
         x_codes = keep.tile([P, T], U32, name="x_codes", align_bytes=64)
         x_scales = keep.tile([P, T], U8, name="x_scales", align_bytes=64)
         x_bf = [keep.tile([P, w, PACK], BF16, name=f"x_bf{h}", align_bytes=64) for h, w in enumerate(NODE_CHUNKS)]
-
-        nc.vector.tensor_copy(wb[:], wb_raw[:].rearrange("p (q r b) -> p r q b", r=PACK, b=2))
-        nc.vector.tensor_copy(sb[:], sb_raw[:].rearrange("p (q r) -> p r q", r=PACK))
         for h, cols in enumerate(node_spans):
             nc.vector.tensor_copy(x_bf[h][:], x_raw[h][:].rearrange("p i t -> p t i"))
             nc.vector.quantize_mx(
                 out=x_codes[:, cols].bitcast(FP8X4), scales=x_scales[:, cols], in_=x_bf[h][:].rearrange("p t i -> p (t i)")
             )
-        nc.vector.tensor_copy(wa[:], wa_raw[:].rearrange("p (q r) -> p r q", r=PACK))
-        nc.vector.tensor_copy(sa[:], sa_raw[:].rearrange("p (q r) -> p r q", r=PACK))
 
-        za = [keep.tile([P, T], F32, name=f"za{r}") for r in range(PACK)]
-        zb = keep.tile([P, PACK, T], F32, name="zb")
+        za = keep.tile([P, SLABS, T], F32, name="za")
+        zb = keep.tile([P, SLABS, T], F32, name="zb")
 
-        def product(out, words, scales, cols):
+        def product_b(out, s, cols):
             nc.tensor.matmul_mx(
                 out=out,
-                lhsT=words,
-                lhsT_scale=scales,
+                lhsT=wb[:, 2 * P * s : 2 * P * (s + 1)].bitcast(FP4X4),
+                lhsT_scale=sb[:, P * s : P * (s + 1)],
                 rhs=x_codes[:, cols].bitcast(FP8X4),
                 rhs_scale=x_scales[:, cols],
                 start=True,
                 stop=True,
             )
 
-        wa_words_of = [wa[:, r, :].bitcast(FP8X4) for r in range(PACK)]
-        wb_words_of = [wb[:, r].rearrange("p q b -> p (q b)").bitcast(FP4X4) for r in range(PACK)]
         for h, cols in enumerate(node_spans):
             w = cols.stop - cols.start
             per_bank = 1 if h == len(NODE_CHUNKS) - 1 else T // w
-            for r0 in range(0, PACK, per_bank):
+            for s0 in range(0, SLABS, per_bank):
                 bank = psum.tile([P, per_bank, w], F32, name="bank")
                 for i in range(per_bank):
-                    product(bank[:, i, :], wb_words_of[r0 + i], sb[:, r0 + i, :], cols)
-                nc.scalar.copy(zb[:, r0 : r0 + per_bank, cols], bank[:])
-        last = node_spans[-1]
-        for r in range(PACK):
-            bank = psum.tile([P, last.start], F32, name="bank")
-            for cols in node_spans[:-1]:
-                product(bank[:, cols], wa_words_of[r], sa[:, r, :], cols)
-            nc.scalar.copy(za[r][:, 0 : last.start], bank[:])
-        bank = psum.tile([P, PACK, T - last.start], F32, name="bank")
-        for r in range(PACK):
-            product(bank[:, r, :], wa_words_of[r], sa[:, r, :], last)
-        for r in range(PACK):
-            nc.scalar.copy(za[r][:, last], bank[:, r, :])
+                    product_b(bank[:, i, :], s0 + i, cols)
+                if h == len(NODE_CHUNKS) - 2:
+                    nc.vector.tensor_scalar(zb[:, s0 : s0 + per_bank, cols], bank[:], -1.0, None, ALU.mult)
+                else:
+                    nc.scalar.activation(zb[:, s0 : s0 + per_bank, cols], bank[:], ACT.Copy, scale=-1.0)
+        for s0 in range(0, SLABS, 2):
+            for cols in spans((T // 2, T // 2)):
+                bank = psum.tile([P, 2, T // 2], F32, name="bank")
+                for i in range(2):
+                    nc.tensor.matmul_mx(
+                        out=bank[:, i, :],
+                        lhsT=wa[:, P * (s0 + i) : P * (s0 + i + 1)].bitcast(FP8X4),
+                        lhsT_scale=sa[:, P * (s0 + i) : P * (s0 + i + 1)],
+                        rhs=x_codes[:, cols].bitcast(FP8X4),
+                        rhs_scale=x_scales[:, cols],
+                        start=True,
+                        stop=True,
+                    )
+                nc.scalar.copy(za[:, s0 : s0 + 2, cols], bank[:])
 
         y_codes = keep.tile([P, J], U32, name="y_codes", align_bytes=64)
         y_scales = keep.tile([P, J], U8, name="y_scales", align_bytes=64)
         y_rows = out_0.rearrange("(p r) j -> p r j", r=PACK)
         code_rows = out_1[0].rearrange("p j r -> p (j r)").bitcast(I32)
 
-        def block(name):
-            return keep.tile([P, PACK, P], F32, name=name)
+        def blocks(name, nb):
+            return keep.tile([P, nb, SLABS, P], F32, name=name)
 
-        def pick(out, b0, nb):
-            for r in range(PACK):
-                nc.vector.tensor_copy(out[:, r, :], zb[:, r, :].indirect(heads[:, 8 * b0 : 8 * (b0 + nb)]))
+        def flat(t):
+            return t.rearrange("p b s j -> p (b s j)")
 
-        def differ(d, picked, b):
-            for r in range(PACK):
-                nc.vector.tensor_tensor(d[:, r, :], za[r][:].indirect(tails[:, 8 * b : 8 * (b + 1)]), picked[:, r, :], ALU.subtract)
+        def pick(out, z, s, lst, b0, nb):
+            nc.vector.tensor_copy(out, z[:, s, :].indirect(lst[:, 8 * b0 : 8 * (b0 + nb)]))
 
-        def soften(b, d, groups):
-            a = block(f"a{b}")
-            s = block(f"s{b}")
-            for rows in groups:
-                nc.scalar.activation(a[:, rows, :], d[:, rows, :], ACT.Abs)
-                nc.scalar.activation(s[:, rows, :], a[:, rows, :], ACT.Abs_reciprocal_sqrt, bias=1.0)
-            return s
+        def soften(ga, gb, nb, slabs, a, sq):
+            bank = psum.tile([P, nb, len(slabs), P], F32, name="bank")
+            for i, s in enumerate(slabs):
+                for b in range(nb):
+                    cols = slice(P * b, P * (b + 1))
+                    nc.tensor.matmul(bank[:, b, i, :], gb[s][:, cols], ident[:], start=True, stop=False, is_transpose=True)
+                    nc.tensor.matmul(bank[:, b, i, :], ga[s][:, cols], ident[:], start=False, stop=True, is_transpose=True)
+            qs = slice(32 * slabs[0], 32 * (slabs[-1] + 1))
+            nc.scalar.activation(a[:, :, :, qs], bank[:].rearrange("p b s (q r) -> p b r (s q)", r=PACK), ACT.Abs)
+            nc.scalar.activation(sq[:, :, :, qs], a[:, :, :, qs], ACT.Abs_reciprocal_sqrt, bias=1.0)
 
-        def scale(b, d, s, groups):
-            v = block(f"v{b}")
-            for rows in groups:
-                nc.vector.tensor_tensor(v[:, rows, :], d[:, rows, :], s[:, rows, :], ALU.mult)
-            return v
+        def scale(v, a, sq, slabs):
+            qs = slice(32 * slabs[0], 32 * (slabs[-1] + 1))
+            nc.vector.tensor_tensor(v[:, :, :, qs], a[:, :, :, qs], sq[:, :, :, qs], ALU.mult)
 
-        def planes(b, v):
+        def finish(b, v, cast_on_vector):
             edges = slice(P * b, P * (b + 1))
+            y = keep.tile([P, PACK, P], F32, name=f"y{b}")
             y_bf = keep.tile([P, P, PACK], BF16, name=f"y_bf{b}", align_bytes=64)
-            nc.scalar.activation(y_bf[:], v[:].rearrange("p r j -> p j r"), ACT.Square)
+            bank = psum.tile([P, PACK, P], F32, name="bank")
+            for r in range(PACK):
+                nc.tensor.transpose(bank[:, r, :], v[:, r, :], ident[:])
+            if cast_on_vector:
+                nc.scalar.activation(y[:], bank[:], ACT.Square)
+                nc.vector.tensor_copy(y_bf[:], y[:].rearrange("p r j -> p j r"))
+            else:
+                nc.scalar.activation(y_bf[:], bank[:].rearrange("p r j -> p j r"), ACT.Square)
+                nc.scalar.activation(y[:], bank[:], ACT.Square)
+            nc.sync.dma_start(y_rows[:, :, edges], y[:])
             nc.vector.quantize_mx(
                 out=y_codes[:, edges].bitcast(FP8X4), scales=y_scales[:, edges], in_=y_bf[:].rearrange("p j r -> p (j r)")
             )
             nc.sync.dma_start(code_rows[:, edges], y_codes[:, edges].bitcast(I32))
 
-        def energy(b, v, on_vector):
-            y = block(f"y{b}")
-            if on_vector:
-                nc.vector.tensor_tensor(y[:], v[:], v[:], ALU.mult)
-            else:
-                nc.scalar.activation(y[:], v[:], ACT.Square)
-            nc.sync.dma_start(y_rows[:, :, P * b : P * (b + 1)], y[:])
-
-        whole = [slice(0, PACK)]
-        split = [slice(0, PACK - 1), slice(PACK - 1, PACK)]
-        p01 = keep.tile([P, PACK, 2 * P], F32, name="p01")
-        d0, d1, d3 = block("d0"), block("d1"), block("d3")
-        pick(p01, 0, 2)
-        differ(d0, p01[:, :, 0:P], 0)
-        s0 = soften(0, d0, whole)
-        differ(d1, p01[:, :, P : 2 * P], 1)
-        s1 = soften(1, d1, whole)
-        v0 = scale(0, d0, s0, whole)
-        planes(0, v0)
-        energy(0, v0, False)
-        pick(s0, 2, 1)
-        v1 = scale(1, d1, s1, whole)
-        planes(1, v1)
-        energy(1, v1, False)
-        differ(s1, s0, 2)
-        s2 = soften(2, s1, whole)
-        pick(s0, 3, 1)
-        differ(d3, s0, 3)
-        s3 = soften(3, d3, split)
-        v2 = scale(2, s1, s2, whole)
-        v3 = scale(3, d3, s3, split)
-        planes(2, v2)
-        planes(3, v3)
-        energy(3, v3, True)
-        energy(2, v2, True)
+        W = 2 * P
+        gb01_t = keep.tile([P, SLABS, W], F32, name="gb01")
+        ga01_t = keep.tile([P, SLABS, W], F32, name="ga01")
+        gb01 = [gb01_t[:, s, :] for s in range(SLABS)]
+        ga01 = [ga01_t[:, s, :] for s in range(SLABS)]
+        a01, sq01, v01 = blocks("a01", 2), blocks("sq01", 2), blocks("v01", 2)
+        a2, sq2, v2 = blocks("a2", 1), blocks("sq2", 1), blocks("v2", 1)
+        a3, sq3, v3 = blocks("a3", 1), blocks("sq3", 1), blocks("v3", 1)
+        gb23 = [gb01[2], gb01[3], flat(sq01[:])[:, 0:W], flat(sq01[:])[:, W : 2 * W]]
+        ga2 = [flat(a01[:])[:, P * s : P * (s + 1)] for s in range(SLABS)]
+        ga3 = [flat(a01[:])[:, P * (SLABS + s) : P * (SLABS + s + 1)] for s in range(SLABS)]
+        for s in range(SLABS):
+            pick(gb01[s], zb, s, heads, 0, 2)
+        for pair in ((0, 1), (2, 3)):
+            for s in pair:
+                pick(ga01[s], za, s, tails, 0, 2)
+            soften(ga01, gb01, 2, pair, a01, sq01)
+        for s in (0, 1):
+            pick(gb23[s], zb, s, heads, 2, 2)
+        for pair in ((0, 1), (2, 3)):
+            scale(v01, a01, sq01, pair)
+        finish(0, v01[:, 0], False)
+        finish(1, v01[:, 1], False)
+        for s in (2, 3):
+            pick(gb23[s], zb, s, heads, 2, 2)
+        for s in range(SLABS):
+            pick(ga2[s], za, s, tails, 2, 1)
+        soften(ga2, [g[:, 0:P] for g in gb23], 1, (0, 1, 2, 3), a2, sq2)
+        for group in ((0, 1), (2,), (3,)):
+            for s in group:
+                pick(ga3[s], za, s, tails, 3, 1)
+            soften(ga3, [g[:, P:W] for g in gb23], 1, group, a3, sq3)
+        scale(v2, a2, sq2, (0, 1, 2, 3))
+        for group in ((0, 1), (2,), (3,)):
+            scale(v3, a3, sq3, group)
+        finish(2, v2[:, 0], True)
+        finish(3, v3[:, 0], False)
         for q in range(4):
             nc.scalar.dma_start(out_2[0, 4 * q : 4 * q + 4, :].bitcast(I32), y_scales[32 * q : 32 * q + 4, :].bitcast(I32))

@@ -21,7 +21,8 @@ P = 128
 PACK = 4
 SLABS = N // P
 BLOCKS = J // P
-NODE_CHUNKS = (128, 128, 128, 128)
+SPARE = 192
+NODE_CHUNKS = (256, 256)
 
 
 def spans(widths):
@@ -54,14 +55,14 @@ def tile_list_edge_difference_energy_pl_kernel(
         wa = keep.tile([P, N], I32, name="wa", align_bytes=64)
         wb = keep.tile([P, 2 * N], U8, name="wb", align_bytes=64)
 
+        nc.sync.dma_start(x_raw[0][:], x_rows[:, :, node_spans[0]])
         nc.sync.dma_start(wb[:].bitcast(I32), wb_words[0].bitcast(I32))
         for q in range(4):
             nc.scalar.dma_start(sb[32 * q : 32 * q + 4, :].bitcast(I32), wb_scales[0, 4 * q : 4 * q + 4, :].bitcast(I32))
-        for h, cols in enumerate(node_spans):
-            nc.sync.dma_start(x_raw[h][:], x_rows[:, :, cols])
+        nc.sync.dma_start(heads[:], offs2)
+        nc.sync.dma_start(x_raw[1][:], x_rows[:, :, node_spans[1]])
         nc.scalar.activation(warm[:], one[:], ACT.Abs_reciprocal_sqrt)
         nc.sync.dma_start(wa[:], wa_words[0].rearrange("p n r -> p (n r)").bitcast(I32))
-        nc.sync.dma_start(heads[:], offs2)
         for q in range(4):
             nc.sync.dma_start(sa[32 * q : 32 * q + 4, :].bitcast(I32), wa_scales[0, 4 * q : 4 * q + 4, :].bitcast(I32))
         nc.sync.dma_start(tails[:], offs)
@@ -70,50 +71,55 @@ def tile_list_edge_difference_energy_pl_kernel(
         x_scales = keep.tile([P, T], U8, name="x_scales", align_bytes=64)
         x_bf = [keep.tile([P, w, PACK], BF16, name=f"x_bf{h}", align_bytes=64) for h, w in enumerate(NODE_CHUNKS)]
         for h, cols in enumerate(node_spans):
-            nc.vector.tensor_copy(x_bf[h][:], x_raw[h][:].rearrange("p i t -> p t i"))
+            by_node = x_raw[h][:].rearrange("p i t -> p t i")
+            nc.vector.tensor_copy(x_bf[h][:, 0:176, :], by_node[:, 0:176, :])
+            nc.scalar.copy(x_bf[h][:, 176:, :], by_node[:, 176:, :])
             nc.vector.quantize_mx(
                 out=x_codes[:, cols].bitcast(FP8X4), scales=x_scales[:, cols], in_=x_bf[h][:].rearrange("p t i -> p (t i)")
             )
 
-        za = keep.tile([P, SLABS, T], F32, name="za")
-        zb = keep.tile([P, SLABS, T], F32, name="zb")
+        za_t = keep.tile([P, SLABS, T], F32, name="za")
+        zb_t = keep.tile([P, SLABS * T + SPARE], F32, name="zb")
+        nc.gpsimd.memset(zb_t[:, SLABS * T :], 0.0)
+        zb_rows = zb_t[:, 0 : SLABS * T].rearrange("p (s t) -> p s t", t=T)
+        place = [SLABS - 1 - s for s in range(SLABS)]
+        za = [za_t[:, s, :] for s in range(SLABS)]
+        zb = [zb_rows[:, place[s], :] for s in range(SLABS)]
+        zb_wide = [zb_t[:, place[s] * T : (place[s] + 1) * T + SPARE] for s in range(SLABS)]
 
-        def product_b(out, s, cols):
+        def product(out, words, scales, cols):
             nc.tensor.matmul_mx(
                 out=out,
-                lhsT=wb[:, 2 * P * s : 2 * P * (s + 1)].bitcast(FP4X4),
-                lhsT_scale=sb[:, P * s : P * (s + 1)],
+                lhsT=words,
+                lhsT_scale=scales,
                 rhs=x_codes[:, cols].bitcast(FP8X4),
                 rhs_scale=x_scales[:, cols],
                 start=True,
                 stop=True,
             )
 
-        for h, cols in enumerate(node_spans):
-            w = cols.stop - cols.start
-            per_bank = 1 if h == len(NODE_CHUNKS) - 1 else T // w
-            for s0 in range(0, SLABS, per_bank):
-                bank = psum.tile([P, per_bank, w], F32, name="bank")
-                for i in range(per_bank):
-                    product_b(bank[:, i, :], s0 + i, cols)
-                if h == len(NODE_CHUNKS) - 2:
-                    nc.vector.tensor_scalar(zb[:, s0 : s0 + per_bank, cols], bank[:], -1.0, None, ALU.mult)
-                else:
-                    nc.scalar.activation(zb[:, s0 : s0 + per_bank, cols], bank[:], ACT.Copy, scale=-1.0)
-        for s0 in range(0, SLABS, 2):
-            for cols in spans((T // 2, T // 2)):
-                bank = psum.tile([P, 2, T // 2], F32, name="bank")
-                for i in range(2):
-                    nc.tensor.matmul_mx(
-                        out=bank[:, i, :],
-                        lhsT=wa[:, P * (s0 + i) : P * (s0 + i + 1)].bitcast(FP8X4),
-                        lhsT_scale=sa[:, P * (s0 + i) : P * (s0 + i + 1)],
-                        rhs=x_codes[:, cols].bitcast(FP8X4),
-                        rhs_scale=x_scales[:, cols],
-                        start=True,
-                        stop=True,
-                    )
-                nc.scalar.copy(za[:, s0 : s0 + 2, cols], bank[:])
+        def product_b(out, s, cols):
+            product(out, wb[:, 2 * P * s : 2 * P * (s + 1)].bitcast(FP4X4), sb[:, P * s : P * (s + 1)], cols)
+
+        first, second = node_spans
+        for s0 in (0, 2):
+            bank = psum.tile([P, 2, T // 2], F32, name="bank")
+            for s in (s0, s0 + 1):
+                product_b(bank[:, s0 + 1 - s, :], s, first)
+            rows = zb_rows[:, place[s0 + 1] : place[s0] + 1, first]
+            if s0 == 0:
+                nc.scalar.activation(rows, bank[:], ACT.Copy, scale=-1.0)
+            else:
+                nc.vector.tensor_scalar(rows, bank[:], -1.0, None, ALU.mult)
+        for s in range(SLABS):
+            bank = psum.tile([P, T // 2], F32, name="bank")
+            product_b(bank[:], s, second)
+            nc.scalar.activation(zb[s][:, second], bank[:], ACT.Copy, scale=-1.0)
+        for cols in spans((P,) * (T // P)):
+            bank = psum.tile([P, SLABS, P], F32, name="bank")
+            for s in range(SLABS):
+                product(bank[:, s, :], wa[:, P * s : P * (s + 1)].bitcast(FP8X4), sa[:, P * s : P * (s + 1)], cols)
+            nc.scalar.copy(za_t[:, :, cols], bank[:])
 
         y_codes = keep.tile([P, J], U32, name="y_codes", align_bytes=64)
         y_scales = keep.tile([P, J], U8, name="y_scales", align_bytes=64)
@@ -127,7 +133,7 @@ def tile_list_edge_difference_energy_pl_kernel(
             return t.rearrange("p b s j -> p (b s j)")
 
         def pick(out, z, s, lst, b0, nb):
-            nc.vector.tensor_copy(out, z[:, s, :].indirect(lst[:, 8 * b0 : 8 * (b0 + nb)]))
+            nc.vector.tensor_copy(out, z[s].indirect(lst[:, 8 * b0 : 8 * (b0 + nb)]))
 
         def soften(ga, gb, nb, slabs, a, sq):
             bank = psum.tile([P, nb, len(slabs), P], F32, name="bank")
@@ -144,61 +150,76 @@ def tile_list_edge_difference_energy_pl_kernel(
             qs = slice(32 * slabs[0], 32 * (slabs[-1] + 1))
             nc.vector.tensor_tensor(v[:, :, :, qs], a[:, :, :, qs], sq[:, :, :, qs], ALU.mult)
 
-        def finish(b, v, cast_on_vector):
-            edges = slice(P * b, P * (b + 1))
-            y = keep.tile([P, PACK, P], F32, name=f"y{b}")
-            y_bf = keep.tile([P, P, PACK], BF16, name=f"y_bf{b}", align_bytes=64)
+        def turn_back(v):
             bank = psum.tile([P, PACK, P], F32, name="bank")
             for r in range(PACK):
                 nc.tensor.transpose(bank[:, r, :], v[:, r, :], ident[:])
-            if cast_on_vector:
-                nc.scalar.activation(y[:], bank[:], ACT.Square)
-                nc.vector.tensor_copy(y_bf[:], y[:].rearrange("p r j -> p j r"))
-            else:
-                nc.scalar.activation(y_bf[:], bank[:].rearrange("p r j -> p j r"), ACT.Square)
-                nc.scalar.activation(y[:], bank[:], ACT.Square)
-            nc.sync.dma_start(y_rows[:, :, edges], y[:])
+            return bank
+
+        def planes(y_bf, edges):
             nc.vector.quantize_mx(
                 out=y_codes[:, edges].bitcast(FP8X4), scales=y_scales[:, edges], in_=y_bf[:].rearrange("p j r -> p (j r)")
             )
             nc.sync.dma_start(code_rows[:, edges], y_codes[:, edges].bitcast(I32))
 
         W = 2 * P
-        gb01_t = keep.tile([P, SLABS, W], F32, name="gb01")
-        ga01_t = keep.tile([P, SLABS, W], F32, name="ga01")
-        gb01 = [gb01_t[:, s, :] for s in range(SLABS)]
-        ga01 = [ga01_t[:, s, :] for s in range(SLABS)]
+        gb_all = keep.tile([P, 2, J], F32, name="gb_all")
+        gb_low = keep.tile([P, 2, W], F32, name="gb_low")
+        ga_low = keep.tile([P, SLABS, W], F32, name="ga_low")
+        ga_high = keep.tile([P, 2, W], F32, name="ga_high")
         a01, sq01, v01 = blocks("a01", 2), blocks("sq01", 2), blocks("v01", 2)
-        a2, sq2, v2 = blocks("a2", 1), blocks("sq2", 1), blocks("v2", 1)
-        a3, sq3, v3 = blocks("a3", 1), blocks("sq3", 1), blocks("v3", 1)
-        gb23 = [gb01[2], gb01[3], flat(sq01[:])[:, 0:W], flat(sq01[:])[:, W : 2 * W]]
-        ga2 = [flat(a01[:])[:, P * s : P * (s + 1)] for s in range(SLABS)]
-        ga3 = [flat(a01[:])[:, P * (SLABS + s) : P * (SLABS + s + 1)] for s in range(SLABS)]
-        for s in range(SLABS):
+        a23, v23 = blocks("a23", 2), blocks("v23", 2)
+        sq23 = keep.tile([P, 2, SLABS, P], F32, name="sq23", tag="late", align_bytes=64)
+        gb01 = [gb_all[:, 0, 0:W], gb_all[:, 1, 0:W], gb_low[:, 0, :], gb_low[:, 1, :]]
+        ga01 = [ga_low[:, s, :] for s in range(SLABS)]
+        gb23 = [gb_all[:, 0, W:J], gb_all[:, 1, W:J], flat(sq01[:])[:, 0:W], flat(sq01[:])[:, W : 2 * W]]
+        ga23 = [ga_high[:, 0, :], ga_high[:, 1, :], flat(a01[:])[:, 0:W], flat(a01[:])[:, W : 2 * W]]
+        for s in (0, 1):
+            pick(gb_all[:, s, :], zb_wide, s, heads, 0, 4)
+        for s in (2, 3):
             pick(gb01[s], zb, s, heads, 0, 2)
         for pair in ((0, 1), (2, 3)):
             for s in pair:
                 pick(ga01[s], za, s, tails, 0, 2)
             soften(ga01, gb01, 2, pair, a01, sq01)
         for s in (0, 1):
-            pick(gb23[s], zb, s, heads, 2, 2)
+            pick(ga23[s], za, s, tails, 2, 2)
+        soften(ga23, gb23, 2, (0, 1), a23, sq23)
         for pair in ((0, 1), (2, 3)):
             scale(v01, a01, sq01, pair)
-        finish(0, v01[:, 0], False)
-        finish(1, v01[:, 1], False)
+        y01 = keep.tile([P, PACK, W], F32, name="y01")
+        y0_bf = keep.tile([P, P, PACK], BF16, name="y0_bf", align_bytes=64)
+        for b in (0, 1):
+            bank = turn_back(v01[:, b])
+            nc.scalar.activation(y01[:, :, P * b : P * (b + 1)], bank[:], ACT.Square)
+            if b == 0:
+                nc.scalar.activation(y0_bf[:], bank[:].rearrange("p r j -> p j r"), ACT.Square)
+        nc.sync.dma_start(y_rows[:, :, 0:W], y01[:])
         for s in (2, 3):
             pick(gb23[s], zb, s, heads, 2, 2)
-        for s in range(SLABS):
-            pick(ga2[s], za, s, tails, 2, 1)
-        soften(ga2, [g[:, 0:P] for g in gb23], 1, (0, 1, 2, 3), a2, sq2)
-        for group in ((0, 1), (2,), (3,)):
-            for s in group:
-                pick(ga3[s], za, s, tails, 3, 1)
-            soften(ga3, [g[:, P:W] for g in gb23], 1, group, a3, sq3)
-        scale(v2, a2, sq2, (0, 1, 2, 3))
-        for group in ((0, 1), (2,), (3,)):
-            scale(v3, a3, sq3, group)
-        finish(2, v2[:, 0], True)
-        finish(3, v3[:, 0], False)
+        for s in (2, 3):
+            pick(ga23[s][:, 0:P], za, s, tails, 2, 1)
+        soften(ga23, gb23, 1, (2, 3), a23[:, 0:1], sq23[:, 0:1])
+        for s in (2, 3):
+            pick(ga23[s][:, P:W], za, s, tails, 3, 1)
+        soften([g[:, P:W] for g in ga23], [g[:, P:W] for g in gb23], 1, (2, 3), a23[:, 1:2], sq23[:, 1:2])
+        scale(v23, a23, sq23, (0, 1))
+        for b in (0, 1):
+            scale(v23[:, b : b + 1], a23[:, b : b + 1], sq23[:, b : b + 1], (2, 3))
+        planes(y0_bf, slice(0, P))
+        y12_bf = keep.tile([P, W, PACK], BF16, name="y12_bf", tag="late", align_bytes=64)
+        y3_bf = keep.tile([P, P, PACK], BF16, name="y3_bf", align_bytes=64)
+        y2 = keep.tile([P, PACK, P], F32, name="y2")
+        y3 = keep.tile([P, PACK, P], F32, name="y3")
+        nc.vector.tensor_copy(y12_bf[:, 0:P, :], y01[:, :, P:W].rearrange("p r j -> p j r"))
+        nc.scalar.activation(y2[:], turn_back(v23[:, 0])[:], ACT.Square)
+        nc.sync.dma_start(y_rows[:, :, W : W + P], y2[:])
+        nc.vector.tensor_copy(y12_bf[:, P:W, :], y2[:].rearrange("p r j -> p j r"))
+        planes(y12_bf, slice(P, W + P))
+        bank = turn_back(v23[:, 1])
+        nc.scalar.activation(y3_bf[:], bank[:].rearrange("p r j -> p j r"), ACT.Square)
+        planes(y3_bf, slice(W + P, J))
+        nc.scalar.activation(y3[:], bank[:], ACT.Square)
+        nc.sync.dma_start(y_rows[:, :, W + P : J], y3[:])
         for q in range(4):
-            nc.scalar.dma_start(out_2[0, 4 * q : 4 * q + 4, :].bitcast(I32), y_scales[32 * q : 32 * q + 4, :].bitcast(I32))
+            nc.sync.dma_start(out_2[0, 4 * q : 4 * q + 4, :].bitcast(I32), y_scales[32 * q : 32 * q + 4, :].bitcast(I32))

@@ -20,13 +20,13 @@ ALU = mybir.AluOpType
 P = 128
 PACK = 4
 SLABS = N // P
-BLOCKS = J // P
+QUADRANTS = 4
+LIST_COLS = P // 16
+Q_PER_SLAB = P // PACK
+HALF = T // 2
+PAIR = 2 * P
 SPARE = 192
-NODE_CHUNKS = (256, 256)
-
-
-def spans(widths):
-    return [slice(sum(widths[:c]), sum(widths[: c + 1])) for c in range(len(widths))]
+VECTOR_SHARE = 176
 
 
 def tile_list_edge_difference_energy_pl_kernel(
@@ -39,53 +39,66 @@ def tile_list_edge_difference_energy_pl_kernel(
 
         tails = keep.tile([P, J // 16], U16, name="tails")
         heads = keep.tile([P, J // 16], U16, name="heads")
-
         sa = keep.tile([P, N], U8, name="sa", align_bytes=64)
         sb = keep.tile([P, N], U8, name="sb", align_bytes=64)
+        wa = keep.tile([P, N], I32, name="wa", align_bytes=64)
+        wb = keep.tile([P, 2 * N], U8, name="wb", align_bytes=64)
+        x_raw = [keep.tile([P, PACK, HALF], F32, name=f"x_raw{h}") for h in range(2)]
 
         one = keep.tile([P, 1], F32, name="one")
-        warm = keep.tile([P, 1], F32, name="warm")
         nc.gpsimd.memset(one[:], 1.0)
         ident = keep.tile([P, P], F32, name="ident")
         make_identity(nc, ident[:])
 
-        x_rows = xt.rearrange("(p i) t -> p i t", i=PACK)
-        node_spans = spans(NODE_CHUNKS)
-        x_raw = [keep.tile([P, PACK, w], F32, name=f"x_raw{h}") for h, w in enumerate(NODE_CHUNKS)]
-        wa = keep.tile([P, N], I32, name="wa", align_bytes=64)
-        wb = keep.tile([P, 2 * N], U8, name="wb", align_bytes=64)
+        za_all = keep.tile([P, SLABS, T], F32, name="za_all")
+        zb_all = keep.tile([P, SLABS * T + SPARE], F32, name="zb_all")
+        zb_rows = zb_all[:, 0 : SLABS * T].rearrange("p (s t) -> p s t", t=T)
+        zb_row = [SLABS - 1 - s for s in range(SLABS)]
+        za = [za_all[:, s, :] for s in range(SLABS)]
+        zb = [zb_rows[:, zb_row[s], :] for s in range(SLABS)]
+        zb_wide = [zb_all[:, zb_row[s] * T : (zb_row[s] + 1) * T + SPARE] for s in range(SLABS)]
 
-        nc.sync.dma_start(x_raw[0][:], x_rows[:, :, node_spans[0]])
+        def live_rows(tile, quad):
+            return tile[32 * quad : 32 * quad + 4, :].bitcast(I32)
+
+        def scale_rows(scales, quad):
+            return scales[0, 4 * quad : 4 * quad + 4, :].bitcast(I32)
+
+        x_rows = xt.rearrange("(p i) t -> p i t", i=PACK)
+        first, second = slice(0, HALF), slice(HALF, T)
+        for quad in range(QUADRANTS):
+            queue = nc.sync if quad == 0 else nc.scalar
+            queue.dma_start(live_rows(sb, quad), scale_rows(wb_scales, quad))
+        nc.sync.dma_start(x_raw[0][:], x_rows[:, :, first])
         nc.sync.dma_start(wb[:].bitcast(I32), wb_words[0].bitcast(I32))
-        for q in range(4):
-            nc.scalar.dma_start(sb[32 * q : 32 * q + 4, :].bitcast(I32), wb_scales[0, 4 * q : 4 * q + 4, :].bitcast(I32))
+        nc.sync.dma_start(x_raw[1][:], x_rows[:, :, second])
         nc.sync.dma_start(heads[:], offs2)
-        nc.sync.dma_start(x_raw[1][:], x_rows[:, :, node_spans[1]])
-        nc.scalar.activation(warm[:], one[:], ACT.Abs_reciprocal_sqrt)
-        nc.sync.dma_start(wa[:], wa_words[0].rearrange("p n r -> p (n r)").bitcast(I32))
-        for q in range(4):
-            nc.sync.dma_start(sa[32 * q : 32 * q + 4, :].bitcast(I32), wa_scales[0, 4 * q : 4 * q + 4, :].bitcast(I32))
+        nc.scalar.activation(zb_all[:, SLABS * T :], one[:].to_broadcast([P, SPARE]), ACT.Abs_reciprocal_sqrt)
+        nc.sync.dma_start(wa[:], wa_words[0].rearrange("p n i -> p (n i)").bitcast(I32))
+        for quad in range(QUADRANTS):
+            nc.sync.dma_start(live_rows(sa, quad), scale_rows(wa_scales, quad))
         nc.sync.dma_start(tails[:], offs)
 
         x_codes = keep.tile([P, T], U32, name="x_codes", align_bytes=64)
         x_scales = keep.tile([P, T], U8, name="x_scales", align_bytes=64)
-        x_bf = [keep.tile([P, w, PACK], BF16, name=f"x_bf{h}", align_bytes=64) for h, w in enumerate(NODE_CHUNKS)]
-        for h, cols in enumerate(node_spans):
-            by_node = x_raw[h][:].rearrange("p i t -> p t i")
-            nc.vector.tensor_copy(x_bf[h][:, 0:176, :], by_node[:, 0:176, :])
-            nc.scalar.copy(x_bf[h][:, 176:, :], by_node[:, 176:, :])
+        x_bf = [keep.tile([P, HALF, PACK], BF16, name=f"x_bf{h}", align_bytes=64) for h in range(2)]
+        by_node = [raw[:].rearrange("p i t -> p t i") for raw in x_raw]
+
+        def quantise_x(h, c0, c1):
+            cols = slice(HALF * h + c0, HALF * h + c1)
             nc.vector.quantize_mx(
-                out=x_codes[:, cols].bitcast(FP8X4), scales=x_scales[:, cols], in_=x_bf[h][:].rearrange("p t i -> p (t i)")
+                out=x_codes[:, cols].bitcast(FP8X4),
+                scales=x_scales[:, cols],
+                in_=x_bf[h][:, c0:c1, :].rearrange("p t i -> p (t i)"),
             )
 
-        za_t = keep.tile([P, SLABS, T], F32, name="za")
-        zb_t = keep.tile([P, SLABS * T + SPARE], F32, name="zb")
-        nc.gpsimd.memset(zb_t[:, SLABS * T :], 0.0)
-        zb_rows = zb_t[:, 0 : SLABS * T].rearrange("p (s t) -> p s t", t=T)
-        place = [SLABS - 1 - s for s in range(SLABS)]
-        za = [za_t[:, s, :] for s in range(SLABS)]
-        zb = [zb_rows[:, place[s], :] for s in range(SLABS)]
-        zb_wide = [zb_t[:, place[s] * T : (place[s] + 1) * T + SPARE] for s in range(SLABS)]
+        nc.vector.tensor_copy(x_bf[0][:, 0:VECTOR_SHARE, :], by_node[0][:, 0:VECTOR_SHARE, :])
+        nc.scalar.copy(x_bf[0][:, VECTOR_SHARE:, :], by_node[0][:, VECTOR_SHARE:, :])
+        quantise_x(0, 0, HALF)
+        for c0 in (0, P):
+            nc.vector.tensor_copy(x_bf[1][:, c0 : c0 + P, :], by_node[1][:, c0 : c0 + P, :])
+        for c0 in (0, P):
+            quantise_x(1, c0, c0 + P)
 
         def product(out, words, scales, cols):
             nc.tensor.matmul_mx(
@@ -101,54 +114,47 @@ def tile_list_edge_difference_energy_pl_kernel(
         def product_b(out, s, cols):
             product(out, wb[:, 2 * P * s : 2 * P * (s + 1)].bitcast(FP4X4), sb[:, P * s : P * (s + 1)], cols)
 
-        first, second = node_spans
-        for s0 in (0, 2):
-            bank = psum.tile([P, 2, T // 2], F32, name="bank")
-            for s in (s0, s0 + 1):
-                product_b(bank[:, s0 + 1 - s, :], s, first)
-            rows = zb_rows[:, place[s0 + 1] : place[s0] + 1, first]
-            if s0 == 0:
-                nc.scalar.activation(rows, bank[:], ACT.Copy, scale=-1.0)
-            else:
-                nc.vector.tensor_scalar(rows, bank[:], -1.0, None, ALU.mult)
-        for s in range(SLABS):
-            bank = psum.tile([P, T // 2], F32, name="bank")
-            product_b(bank[:], s, second)
-            nc.scalar.activation(zb[s][:, second], bank[:], ACT.Copy, scale=-1.0)
-        for cols in spans((P,) * (T // P)):
+        bank = psum.tile([P, 2, HALF], F32, name="bank")
+        for s in (0, 1):
+            product_b(bank[:, 1 - s, :], s, first)
+        nc.scalar.activation(zb_rows[:, zb_row[1] : zb_row[0] + 1, first], bank[:], ACT.Copy, scale=-1.0)
+        pieces = [(0, slice(HALF, HALF + P)), (0, slice(HALF + P, T)), (1, second), (2, slice(0, T)), (3, slice(0, T))]
+        for s, cols in pieces:
+            bank = psum.tile([P, cols.stop - cols.start], F32, name="bank")
+            product_b(bank[:], s, cols)
+            nc.scalar.activation(zb[s][:, cols], bank[:], ACT.Copy, scale=-1.0)
+        for c0 in range(0, T, P):
+            cols = slice(c0, c0 + P)
             bank = psum.tile([P, SLABS, P], F32, name="bank")
             for s in range(SLABS):
                 product(bank[:, s, :], wa[:, P * s : P * (s + 1)].bitcast(FP8X4), sa[:, P * s : P * (s + 1)], cols)
-            nc.scalar.copy(za_t[:, :, cols], bank[:])
+            nc.scalar.copy(za_all[:, :, cols], bank[:])
 
         y_codes = keep.tile([P, J], U32, name="y_codes", align_bytes=64)
         y_scales = keep.tile([P, J], U8, name="y_scales", align_bytes=64)
         y_rows = out_0.rearrange("(p r) j -> p r j", r=PACK)
         code_rows = out_1[0].rearrange("p j r -> p (j r)").bitcast(I32)
 
-        def blocks(name, nb):
-            return keep.tile([P, nb, SLABS, P], F32, name=name)
+        def pick(out, window, offsets, b0, blocks):
+            nc.vector.tensor_copy(out, window.indirect(offsets[:, LIST_COLS * b0 : LIST_COLS * (b0 + blocks)]))
 
-        def flat(t):
-            return t.rearrange("p b s j -> p (b s j)")
+        def places(slabs):
+            return slice(Q_PER_SLAB * slabs[0], Q_PER_SLAB * (slabs[-1] + 1))
 
-        def pick(out, z, s, lst, b0, nb):
-            nc.vector.tensor_copy(out, z[s].indirect(lst[:, 8 * b0 : 8 * (b0 + nb)]))
-
-        def soften(ga, gb, nb, slabs, a, sq):
-            bank = psum.tile([P, nb, len(slabs), P], F32, name="bank")
+        def soften(ga, gb, blocks, slabs, mag, root):
+            bank = psum.tile([P, blocks, len(slabs), P], F32, name="bank")
             for i, s in enumerate(slabs):
-                for b in range(nb):
+                for b in range(blocks):
                     cols = slice(P * b, P * (b + 1))
                     nc.tensor.matmul(bank[:, b, i, :], gb[s][:, cols], ident[:], start=True, stop=False, is_transpose=True)
                     nc.tensor.matmul(bank[:, b, i, :], ga[s][:, cols], ident[:], start=False, stop=True, is_transpose=True)
-            qs = slice(32 * slabs[0], 32 * (slabs[-1] + 1))
-            nc.scalar.activation(a[:, :, :, qs], bank[:].rearrange("p b s (q r) -> p b r (s q)", r=PACK), ACT.Abs)
-            nc.scalar.activation(sq[:, :, :, qs], a[:, :, :, qs], ACT.Abs_reciprocal_sqrt, bias=1.0)
+            qs = places(slabs)
+            nc.scalar.activation(mag[:, :, :, qs], bank[:].rearrange("p b s (q r) -> p b r (s q)", r=PACK), ACT.Abs)
+            nc.scalar.activation(root[:, :, :, qs], mag[:, :, :, qs], ACT.Abs_reciprocal_sqrt, bias=1.0)
 
-        def scale(v, a, sq, slabs):
-            qs = slice(32 * slabs[0], 32 * (slabs[-1] + 1))
-            nc.vector.tensor_tensor(v[:, :, :, qs], a[:, :, :, qs], sq[:, :, :, qs], ALU.mult)
+        def scale(v, mag, root, slabs):
+            qs = places(slabs)
+            nc.vector.tensor_tensor(v[:, :, :, qs], mag[:, :, :, qs], root[:, :, :, qs], ALU.mult)
 
         def turn_back(v):
             bank = psum.tile([P, PACK, P], F32, name="bank")
@@ -158,68 +164,74 @@ def tile_list_edge_difference_energy_pl_kernel(
 
         def planes(y_bf, edges):
             nc.vector.quantize_mx(
-                out=y_codes[:, edges].bitcast(FP8X4), scales=y_scales[:, edges], in_=y_bf[:].rearrange("p j r -> p (j r)")
+                out=y_codes[:, edges].bitcast(FP8X4),
+                scales=y_scales[:, edges],
+                in_=y_bf[:].rearrange("p j r -> p (j r)"),
             )
             nc.sync.dma_start(code_rows[:, edges], y_codes[:, edges].bitcast(I32))
 
-        W = 2 * P
-        gb_all = keep.tile([P, 2, J], F32, name="gb_all")
-        gb_low = keep.tile([P, 2, W], F32, name="gb_low")
-        ga_low = keep.tile([P, SLABS, W], F32, name="ga_low")
-        ga_high = keep.tile([P, 2, W], F32, name="ga_high")
-        a01, sq01, v01 = blocks("a01", 2), blocks("sq01", 2), blocks("v01", 2)
-        a23, v23 = blocks("a23", 2), blocks("v23", 2)
-        sq23 = keep.tile([P, 2, SLABS, P], F32, name="sq23", tag="late", align_bytes=64)
-        gb01 = [gb_all[:, 0, 0:W], gb_all[:, 1, 0:W], gb_low[:, 0, :], gb_low[:, 1, :]]
+        gb_whole = keep.tile([P, 2, J], F32, name="gb_whole")
+        gb_rest = keep.tile([P, 2, PAIR], F32, name="gb_rest")
+        ga_low = keep.tile([P, SLABS, PAIR], F32, name="ga_low")
+        ga_high = keep.tile([P, 2, PAIR], F32, name="ga_high")
+        mag01, root01, v01, mag23, v23 = [
+            keep.tile([P, 2, PACK, P], F32, name=name) for name in ("mag01", "root01", "v01", "mag23", "v23")
+        ]
+        root23 = keep.tile([P, 2, PACK, P], F32, name="root23", tag="late", align_bytes=64)
+        gb01 = [gb_whole[:, 0, 0:PAIR], gb_whole[:, 1, 0:PAIR], gb_rest[:, 0, :], gb_rest[:, 1, :]]
         ga01 = [ga_low[:, s, :] for s in range(SLABS)]
-        gb23 = [gb_all[:, 0, W:J], gb_all[:, 1, W:J], flat(sq01[:])[:, 0:W], flat(sq01[:])[:, W : 2 * W]]
-        ga23 = [ga_high[:, 0, :], ga_high[:, 1, :], flat(a01[:])[:, 0:W], flat(a01[:])[:, W : 2 * W]]
+        root01_flat = root01[:].rearrange("p b r q -> p (b r q)")
+        mag01_flat = mag01[:].rearrange("p b r q -> p (b r q)")
+        gb23 = [gb_whole[:, 0, PAIR:J], gb_whole[:, 1, PAIR:J], root01_flat[:, 0:PAIR], root01_flat[:, PAIR : 2 * PAIR]]
+        ga23 = [ga_high[:, 0, :], ga_high[:, 1, :], mag01_flat[:, 0:PAIR], mag01_flat[:, PAIR : 2 * PAIR]]
+
         for s in (0, 1):
-            pick(gb_all[:, s, :], zb_wide, s, heads, 0, 4)
+            pick(gb_whole[:, s, :], zb_wide[s], heads, 0, 4)
         for s in (2, 3):
-            pick(gb01[s], zb, s, heads, 0, 2)
-        for pair in ((0, 1), (2, 3)):
-            for s in pair:
-                pick(ga01[s], za, s, tails, 0, 2)
-            soften(ga01, gb01, 2, pair, a01, sq01)
+            pick(gb01[s], zb[s], heads, 0, 2)
+        for slabs in ((0, 1), (2, 3)):
+            for s in slabs:
+                pick(ga01[s], za[s], tails, 0, 2)
+            soften(ga01, gb01, 2, slabs, mag01, root01)
         for s in (0, 1):
-            pick(ga23[s], za, s, tails, 2, 2)
-        soften(ga23, gb23, 2, (0, 1), a23, sq23)
-        for pair in ((0, 1), (2, 3)):
-            scale(v01, a01, sq01, pair)
-        y01 = keep.tile([P, PACK, W], F32, name="y01")
+            pick(ga23[s], za[s], tails, 2, 2)
+        soften(ga23, gb23, 2, (0, 1), mag23, root23)
+        for slabs in ((0, 1), (2, 3)):
+            scale(v01, mag01, root01, slabs)
+
+        y01 = keep.tile([P, PACK, PAIR], F32, name="y01")
         y0_bf = keep.tile([P, P, PACK], BF16, name="y0_bf", align_bytes=64)
+        bank = turn_back(v01[:, 0])
+        nc.scalar.activation(y01[:, :, 0:P], bank[:], ACT.Square)
+        nc.scalar.activation(y0_bf[:], bank[:].rearrange("p r j -> p j r"), ACT.Square)
+        nc.scalar.activation(y01[:, :, P:PAIR], turn_back(v01[:, 1])[:], ACT.Square)
+        nc.sync.dma_start(y_rows[:, :, 0:PAIR], y01[:])
+
+        for s in (2, 3):
+            pick(gb23[s], zb[s], heads, 2, 2)
         for b in (0, 1):
-            bank = turn_back(v01[:, b])
-            nc.scalar.activation(y01[:, :, P * b : P * (b + 1)], bank[:], ACT.Square)
-            if b == 0:
-                nc.scalar.activation(y0_bf[:], bank[:].rearrange("p r j -> p j r"), ACT.Square)
-        nc.sync.dma_start(y_rows[:, :, 0:W], y01[:])
-        for s in (2, 3):
-            pick(gb23[s], zb, s, heads, 2, 2)
-        for s in (2, 3):
-            pick(ga23[s][:, 0:P], za, s, tails, 2, 1)
-        soften(ga23, gb23, 1, (2, 3), a23[:, 0:1], sq23[:, 0:1])
-        for s in (2, 3):
-            pick(ga23[s][:, P:W], za, s, tails, 3, 1)
-        soften([g[:, P:W] for g in ga23], [g[:, P:W] for g in gb23], 1, (2, 3), a23[:, 1:2], sq23[:, 1:2])
-        scale(v23, a23, sq23, (0, 1))
+            cols = slice(P * b, P * (b + 1))
+            for s in (2, 3):
+                pick(ga23[s][:, cols], za[s], tails, 2 + b, 1)
+            soften([g[:, cols] for g in ga23], [g[:, cols] for g in gb23], 1, (2, 3), mag23[:, b : b + 1], root23[:, b : b + 1])
+        scale(v23, mag23, root23, (0, 1))
         for b in (0, 1):
-            scale(v23[:, b : b + 1], a23[:, b : b + 1], sq23[:, b : b + 1], (2, 3))
+            scale(v23[:, b : b + 1], mag23[:, b : b + 1], root23[:, b : b + 1], (2, 3))
+
         planes(y0_bf, slice(0, P))
-        y12_bf = keep.tile([P, W, PACK], BF16, name="y12_bf", tag="late", align_bytes=64)
+        y12_bf = keep.tile([P, PAIR, PACK], BF16, name="y12_bf", tag="late", align_bytes=64)
         y3_bf = keep.tile([P, P, PACK], BF16, name="y3_bf", align_bytes=64)
         y2 = keep.tile([P, PACK, P], F32, name="y2")
         y3 = keep.tile([P, PACK, P], F32, name="y3")
-        nc.vector.tensor_copy(y12_bf[:, 0:P, :], y01[:, :, P:W].rearrange("p r j -> p j r"))
+        nc.vector.tensor_copy(y12_bf[:, 0:P, :], y01[:, :, P:PAIR].rearrange("p r j -> p j r"))
         nc.scalar.activation(y2[:], turn_back(v23[:, 0])[:], ACT.Square)
-        nc.sync.dma_start(y_rows[:, :, W : W + P], y2[:])
-        nc.vector.tensor_copy(y12_bf[:, P:W, :], y2[:].rearrange("p r j -> p j r"))
-        planes(y12_bf, slice(P, W + P))
+        nc.sync.dma_start(y_rows[:, :, 2 * P : 3 * P], y2[:])
+        nc.vector.tensor_copy(y12_bf[:, P:PAIR, :], y2[:].rearrange("p r j -> p j r"))
+        planes(y12_bf, slice(P, 3 * P))
         bank = turn_back(v23[:, 1])
         nc.scalar.activation(y3_bf[:], bank[:].rearrange("p r j -> p j r"), ACT.Square)
-        planes(y3_bf, slice(W + P, J))
+        planes(y3_bf, slice(3 * P, J))
         nc.scalar.activation(y3[:], bank[:], ACT.Square)
-        nc.sync.dma_start(y_rows[:, :, W + P : J], y3[:])
-        for q in range(4):
-            nc.sync.dma_start(out_2[0, 4 * q : 4 * q + 4, :].bitcast(I32), y_scales[32 * q : 32 * q + 4, :].bitcast(I32))
+        nc.sync.dma_start(y_rows[:, :, 3 * P : J], y3[:])
+        for quad in range(QUADRANTS):
+            nc.sync.dma_start(scale_rows(out_2, quad), live_rows(y_scales, quad))

@@ -123,12 +123,12 @@ def tile_list_edge_difference_energy_pl_kernel(
             bank = psum.tile([P, cols.stop - cols.start], F32, name="bank")
             product_b(bank[:], s, cols)
             nc.scalar.activation(zb[s][:, cols], bank[:], ACT.Copy, scale=-1.0)
-        for c0 in range(0, T, P):
-            cols = slice(c0, c0 + P)
-            bank = psum.tile([P, SLABS, P], F32, name="bank")
-            for s in range(SLABS):
-                product(bank[:, s, :], wa[:, P * s : P * (s + 1)].bitcast(FP8X4), sa[:, P * s : P * (s + 1)], cols)
-            nc.scalar.copy(za_all[:, :, cols], bank[:])
+        for cols in (first, second):
+            for s0 in (0, 2):
+                bank = psum.tile([P, 2, HALF], F32, name="bank")
+                for s in (s0, s0 + 1):
+                    product(bank[:, s - s0, :], wa[:, P * s : P * (s + 1)].bitcast(FP8X4), sa[:, P * s : P * (s + 1)], cols)
+                nc.scalar.copy(za_all[:, s0 : s0 + 2, cols], bank[:])
 
         y_codes = keep.tile([P, J], U32, name="y_codes", align_bytes=64)
         y_scales = keep.tile([P, J], U8, name="y_scales", align_bytes=64)
@@ -173,7 +173,6 @@ def tile_list_edge_difference_energy_pl_kernel(
         gb_whole = keep.tile([P, 2, J], F32, name="gb_whole")
         gb_rest = keep.tile([P, 2, PAIR], F32, name="gb_rest")
         ga_low = keep.tile([P, SLABS, PAIR], F32, name="ga_low")
-        ga_high = keep.tile([P, 2, PAIR], F32, name="ga_high")
         mag01, root01, v01, mag23, v23 = [
             keep.tile([P, 2, PACK, P], F32, name=name) for name in ("mag01", "root01", "v01", "mag23", "v23")
         ]
@@ -183,7 +182,7 @@ def tile_list_edge_difference_energy_pl_kernel(
         root01_flat = root01[:].rearrange("p b r q -> p (b r q)")
         mag01_flat = mag01[:].rearrange("p b r q -> p (b r q)")
         gb23 = [gb_whole[:, 0, PAIR:J], gb_whole[:, 1, PAIR:J], root01_flat[:, 0:PAIR], root01_flat[:, PAIR : 2 * PAIR]]
-        ga23 = [ga_high[:, 0, :], ga_high[:, 1, :], mag01_flat[:, 0:PAIR], mag01_flat[:, PAIR : 2 * PAIR]]
+        ga23 = [gb_rest[:, 0, :], gb_rest[:, 1, :], mag01_flat[:, 0:PAIR], mag01_flat[:, PAIR : 2 * PAIR]]
 
         for s in (0, 1):
             pick(gb_whole[:, s, :], zb_wide[s], heads, 0, 4)

from contextlib import ExitStack

import concourse.mybir as mybir
from concourse.masks import make_identity

K, T, J, N = 512, 512, 512, 512
FLOPS = 2 * 2 * K * T * N

F32 = mybir.dt.float32
BF16 = mybir.dt.bfloat16
I32 = mybir.dt.int32
U32 = mybir.dt.uint32
U16 = mybir.dt.uint16
U8 = mybir.dt.uint8
FP8X4 = mybir.dt.float8_e4m3fn_x4
FP4X4 = mybir.dt.float4_e2m1fn_x4
ACT = mybir.ActivationFunctionType
ALU = mybir.AluOpType

P = 128
PACK = 4
SLABS = N // P
QUADRANTS = 4
LIST_COLS = P // 16
Q_PER_SLAB = P // PACK
HALF = T // 2
PAIR = 2 * P
SPARE = 192
VECTOR_SHARE = 176


def tile_list_edge_difference_energy_pl_kernel(
    tc, xt, wa_words, wa_scales, wb_words, wb_scales, offs, offs2, out_0, out_1, out_2
):
    nc = tc.nc
    with ExitStack() as ctx:
        keep = ctx.enter_context(tc.tile_pool(name="keep", bufs=1))
        psum = ctx.enter_context(tc.psum_pool(name="psum", bufs=8))

        tails = keep.tile([P, J // 16], U16, name="tails")
        heads = keep.tile([P, J // 16], U16, name="heads")
        sa = keep.tile([P, N], U8, name="sa", align_bytes=64)
        sb = keep.tile([P, N], U8, name="sb", align_bytes=64)
        wa = keep.tile([P, N], I32, name="wa", align_bytes=64)
        wb = keep.tile([P, 2 * N], U8, name="wb", align_bytes=64)
        x_raw = [keep.tile([P, PACK, HALF], F32, name=f"x_raw{h}") for h in range(2)]

        one = keep.tile([P, 1], F32, name="one")
        nc.gpsimd.memset(one[:], 1.0)
        ident = keep.tile([P, P], F32, name="ident")
        make_identity(nc, ident[:])

        za_all = keep.tile([P, SLABS, T], F32, name="za_all")
        zb_all = keep.tile([P, SLABS * T + SPARE], F32, name="zb_all")
        zb_rows = zb_all[:, 0 : SLABS * T].rearrange("p (s t) -> p s t", t=T)
        zb_row = [SLABS - 1 - s for s in range(SLABS)]
        za = [za_all[:, s, :] for s in range(SLABS)]
        zb = [zb_rows[:, zb_row[s], :] for s in range(SLABS)]
        zb_wide = [zb_all[:, zb_row[s] * T : (zb_row[s] + 1) * T + SPARE] for s in range(SLABS)]

        def live_rows(tile, quad):
            return tile[32 * quad : 32 * quad + 4, :].bitcast(I32)

        def scale_rows(scales, quad):
            return scales[0, 4 * quad : 4 * quad + 4, :].bitcast(I32)

        x_rows = xt.rearrange("(p i) t -> p i t", i=PACK)
        first, second = slice(0, HALF), slice(HALF, T)
        for quad in range(QUADRANTS):
            queue = nc.sync if quad == 0 else nc.scalar
            queue.dma_start(live_rows(sb, quad), scale_rows(wb_scales, quad))
        nc.sync.dma_start(x_raw[0][:], x_rows[:, :, first])
        nc.sync.dma_start(wb[:].bitcast(I32), wb_words[0].bitcast(I32))
        nc.sync.dma_start(x_raw[1][:], x_rows[:, :, second])
        nc.sync.dma_start(heads[:], offs2)
        nc.scalar.activation(zb_all[:, SLABS * T :], one[:].to_broadcast([P, SPARE]), ACT.Abs_reciprocal_sqrt)
        nc.sync.dma_start(wa[:], wa_words[0].rearrange("p n i -> p (n i)").bitcast(I32))
        for quad in range(QUADRANTS):
            nc.sync.dma_start(live_rows(sa, quad), scale_rows(wa_scales, quad))
        nc.sync.dma_start(tails[:], offs)

        x_codes = keep.tile([P, T], U32, name="x_codes", align_bytes=64)
        x_scales = keep.tile([P, T], U8, name="x_scales", align_bytes=64)
        x_bf = [keep.tile([P, HALF, PACK], BF16, name=f"x_bf{h}", align_bytes=64) for h in range(2)]
        by_node = [raw[:].rearrange("p i t -> p t i") for raw in x_raw]

        def quantise_x(h, c0, c1):
            cols = slice(HALF * h + c0, HALF * h + c1)
            nc.vector.quantize_mx(
                out=x_codes[:, cols].bitcast(FP8X4),
                scales=x_scales[:, cols],
                in_=x_bf[h][:, c0:c1, :].rearrange("p t i -> p (t i)"),
            )

        nc.vector.tensor_copy(x_bf[0][:, 0:VECTOR_SHARE, :], by_node[0][:, 0:VECTOR_SHARE, :])
        nc.scalar.copy(x_bf[0][:, VECTOR_SHARE:, :], by_node[0][:, VECTOR_SHARE:, :])
        quantise_x(0, 0, HALF)
        for c0 in (0, P):
            nc.vector.tensor_copy(x_bf[1][:, c0 : c0 + P, :], by_node[1][:, c0 : c0 + P, :])
        for c0 in (0, P):
            quantise_x(1, c0, c0 + P)

        def product(out, words, scales, cols):
            nc.tensor.matmul_mx(
                out=out,
                lhsT=words,
                lhsT_scale=scales,
                rhs=x_codes[:, cols].bitcast(FP8X4),
                rhs_scale=x_scales[:, cols],
                start=True,
                stop=True,
            )

        def product_b(out, s, cols):
            product(out, wb[:, 2 * P * s : 2 * P * (s + 1)].bitcast(FP4X4), sb[:, P * s : P * (s + 1)], cols)

        bank = psum.tile([P, 2, HALF], F32, name="bank")
        for s in (0, 1):
            product_b(bank[:, 1 - s, :], s, first)
        nc.scalar.activation(zb_rows[:, zb_row[1] : zb_row[0] + 1, first], bank[:], ACT.Copy, scale=-1.0)
        pieces = [(0, slice(HALF, HALF + P)), (0, slice(HALF + P, T)), (1, second), (2, slice(0, T)), (3, slice(0, T))]
        for s, cols in pieces:
            bank = psum.tile([P, cols.stop - cols.start], F32, name="bank")
            product_b(bank[:], s, cols)
            nc.scalar.activation(zb[s][:, cols], bank[:], ACT.Copy, scale=-1.0)
        for cols in (first, second):
            for s0 in (0, 2):
                bank = psum.tile([P, 2, HALF], F32, name="bank")
                for s in (s0, s0 + 1):
                    product(bank[:, s - s0, :], wa[:, P * s : P * (s + 1)].bitcast(FP8X4), sa[:, P * s : P * (s + 1)], cols)
                nc.scalar.copy(za_all[:, s0 : s0 + 2, cols], bank[:])

        y_codes = keep.tile([P, J], U32, name="y_codes", align_bytes=64)
        y_scales = keep.tile([P, J], U8, name="y_scales", align_bytes=64)
        y_rows = out_0.rearrange("(p r) j -> p r j", r=PACK)
        code_rows = out_1[0].rearrange("p j r -> p (j r)").bitcast(I32)

        def pick(out, window, offsets, b0, blocks):
            nc.vector.tensor_copy(out, window.indirect(offsets[:, LIST_COLS * b0 : LIST_COLS * (b0 + blocks)]))

        def places(slabs):
            return slice(Q_PER_SLAB * slabs[0], Q_PER_SLAB * (slabs[-1] + 1))

        def soften(ga, gb, blocks, slabs, mag, root):
            bank = psum.tile([P, blocks, len(slabs), P], F32, name="bank")
            for i, s in enumerate(slabs):
                for b in range(blocks):
                    cols = slice(P * b, P * (b + 1))
                    nc.tensor.matmul(bank[:, b, i, :], gb[s][:, cols], ident[:], start=True, stop=False, is_transpose=True)
                    nc.tensor.matmul(bank[:, b, i, :], ga[s][:, cols], ident[:], start=False, stop=True, is_transpose=True)
            qs = places(slabs)
            nc.scalar.activation(mag[:, :, :, qs], bank[:].rearrange("p b s (q r) -> p b r (s q)", r=PACK), ACT.Abs)
            nc.scalar.activation(root[:, :, :, qs], mag[:, :, :, qs], ACT.Abs_reciprocal_sqrt, bias=1.0)

        def scale(v, mag, root, slabs):
            qs = places(slabs)
            nc.vector.tensor_tensor(v[:, :, :, qs], mag[:, :, :, qs], root[:, :, :, qs], ALU.mult)

        def turn_back(v):
            bank = psum.tile([P, PACK, P], F32, name="bank")
            for r in range(PACK):
                nc.tensor.transpose(bank[:, r, :], v[:, r, :], ident[:])
            return bank

        def planes(y_bf, edges):
            nc.vector.quantize_mx(
                out=y_codes[:, edges].bitcast(FP8X4),
                scales=y_scales[:, edges],
                in_=y_bf[:].rearrange("p j r -> p (j r)"),
            )
            nc.sync.dma_start(code_rows[:, edges], y_codes[:, edges].bitcast(I32))

        gb_whole = keep.tile([P, 2, J], F32, name="gb_whole")
        gb_rest = keep.tile([P, 2, PAIR], F32, name="gb_rest")
        ga_low = keep.tile([P, SLABS, PAIR], F32, name="ga_low")
        mag01, root01, v01, mag23, v23 = [
            keep.tile([P, 2, PACK, P], F32, name=name) for name in ("mag01", "root01", "v01", "mag23", "v23")
        ]
        root23 = keep.tile([P, 2, PACK, P], F32, name="root23", tag="late", align_bytes=64)
        gb01 = [gb_whole[:, 0, 0:PAIR], gb_whole[:, 1, 0:PAIR], gb_rest[:, 0, :], gb_rest[:, 1, :]]
        ga01 = [ga_low[:, s, :] for s in range(SLABS)]
        root01_flat = root01[:].rearrange("p b r q -> p (b r q)")
        mag01_flat = mag01[:].rearrange("p b r q -> p (b r q)")
        gb23 = [gb_whole[:, 0, PAIR:J], gb_whole[:, 1, PAIR:J], root01_flat[:, 0:PAIR], root01_flat[:, PAIR : 2 * PAIR]]
        ga23 = [gb_rest[:, 0, :], gb_rest[:, 1, :], mag01_flat[:, 0:PAIR], mag01_flat[:, PAIR : 2 * PAIR]]

        for s in (0, 1):
            pick(gb_whole[:, s, :], zb_wide[s], heads, 0, 4)
        for s in (2, 3):
            pick(gb01[s], zb[s], heads, 0, 2)
        for slabs in ((0, 1), (2, 3)):
            for s in slabs:
                pick(ga01[s], za[s], tails, 0, 2)
            soften(ga01, gb01, 2, slabs, mag01, root01)
        for s in (0, 1):
            pick(ga23[s], za[s], tails, 2, 2)
        soften(ga23, gb23, 2, (0, 1), mag23, root23)
        for slabs in ((0, 1), (2, 3)):
            scale(v01, mag01, root01, slabs)

        y01 = keep.tile([P, PACK, PAIR], F32, name="y01")
        y0_bf = keep.tile([P, P, PACK], BF16, name="y0_bf", align_bytes=64)
        bank = turn_back(v01[:, 0])
        nc.scalar.activation(y01[:, :, 0:P], bank[:], ACT.Square)
        nc.scalar.activation(y0_bf[:], bank[:].rearrange("p r j -> p j r"), ACT.Square)
        nc.scalar.activation(y01[:, :, P:PAIR], turn_back(v01[:, 1])[:], ACT.Square)
        nc.sync.dma_start(y_rows[:, :, 0:PAIR], y01[:])

        for s in (2, 3):
            pick(gb23[s], zb[s], heads, 2, 2)
        for b in (0, 1):
            cols = slice(P * b, P * (b + 1))
            for s in (2, 3):
                pick(ga23[s][:, cols], za[s], tails, 2 + b, 1)
            soften([g[:, cols] for g in ga23], [g[:, cols] for g in gb23], 1, (2, 3), mag23[:, b : b + 1], root23[:, b : b + 1])
        scale(v23, mag23, root23, (0, 1))
        for b in (0, 1):
            scale(v23[:, b : b + 1], mag23[:, b : b + 1], root23[:, b : b + 1], (2, 3))

        planes(y0_bf, slice(0, P))
        y12_bf = keep.tile([P, PAIR, PACK], BF16, name="y12_bf", tag="late", align_bytes=64)
        y3_bf = keep.tile([P, P, PACK], BF16, name="y3_bf", align_bytes=64)
        y2 = keep.tile([P, PACK, P], F32, name="y2")
        y3 = keep.tile([P, PACK, P], F32, name="y3")
        nc.vector.tensor_copy(y12_bf[:, 0:P, :], y01[:, :, P:PAIR].rearrange("p r j -> p j r"))
        nc.scalar.activation(y2[:], turn_back(v23[:, 0])[:], ACT.Square)
        nc.sync.dma_start(y_rows[:, :, 2 * P : 3 * P], y2[:])
        nc.vector.tensor_copy(y12_bf[:, P:PAIR, :], y2[:].rearrange("p r j -> p j r"))
        planes(y12_bf, slice(P, 3 * P))
        bank = turn_back(v23[:, 1])
        nc.scalar.activation(y3_bf[:], bank[:].rearrange("p r j -> p j r"), ACT.Square)
        planes(y3_bf, slice(3 * P, J))
        nc.scalar.activation(y3[:], bank[:], ACT.Square)
        nc.sync.dma_start(y_rows[:, :, 3 * P : J], y3[:])
        for quad in range(QUADRANTS):
            nc.sync.dma_start(scale_rows(out_2, quad), live_rows(y_scales, quad))
